import numpy as np
import ml_dtypes


def mxq(x, axis, fmt="e4m3"):
    dtype, down = {"e4m3": (ml_dtypes.float8_e4m3fn, 7), "e5m2": (ml_dtypes.float8_e5m2, 14)}[fmt]
    v = np.moveaxis(np.asarray(x, np.float32).astype(ml_dtypes.bfloat16).astype(np.float64), axis, -1)
    blocks = v.reshape(v.shape[:-1] + (-1, 32))
    amax = np.abs(blocks).max(-1, keepdims=True)
    byte = np.maximum(np.where(amax > 0, np.frexp(amax)[1] - 1 + 127, 0) - down, 1)
    scale = np.exp2(byte - 127.0)
    codes = (blocks / scale).astype(np.float32).astype(dtype).astype(np.float64)
    return np.moveaxis((codes * scale).reshape(v.shape), -1, axis)


WIDE = False


def mx_kscale(k):
    if not WIDE:
        return np.ones(k)
    levels = np.array([10, -10, 5, -5, 0])
    if k % 512:
        return np.exp2(np.random.permutation(np.resize(levels, k // 32))).repeat(32)
    a = np.empty((k // 512, 16))
    for p in range(k // 512):
        a[p, :8] = np.random.permutation(np.resize(levels, 8))
        for g in range(8):
            far = levels[np.abs(levels - a[p, g]) >= 10]
            a[p, g + 8] = far[np.random.randint(len(far))]
    return np.exp2(a.ravel()).repeat(32)


def f64(x):
    return np.asarray(x).astype(np.float64)


def striped(idx):
    return np.tile(idx.reshape(-1, 16).T, (8, 1)).astype(np.uint16)


def unstriped(offs):
    return offs[:16].T.reshape(-1).astype(np.int64)


E2M1 = np.array([0.0, 0.5, 1.0, 1.5, 2.0, 3.0, 4.0, 6.0, -0.0, -0.5, -1.0, -1.5, -2.0, -3.0, -4.0, -6.0])


def pack_weight(w, fmt):
    k, n = w.shape
    w = f64(np.asarray(w, np.float32).astype(ml_dtypes.bfloat16)).reshape(k // 32, 32, n)
    amax = np.abs(w).max(1)
    if fmt == "e4m3":
        byte = np.frexp(amax)[1] - 1 + 127 - 7
    else:
        mant, ex = np.frexp(amax / 6.0)
        byte = np.where(mant > 0.5, ex, ex - 1) + 127
    byte = np.clip(np.where(amax > 0, byte, 1), 1, 254)
    scaled = (w * np.exp2(127.0 - byte)[:, None, :]).reshape(k, n).astype(np.float32)
    by_word = np.ascontiguousarray(scaled.reshape(k // 512, 128, 4, n).transpose(0, 1, 3, 2))
    if fmt == "e4m3":
        words = by_word.astype(ml_dtypes.float8_e4m3fn).view(np.uint8)
    else:
        c = by_word.astype(ml_dtypes.float4_e2m1fn).view(np.uint8) & 0xF
        words = (c[..., 0::2] | (c[..., 1::2] << 4)).reshape(k // 512, 128, 2 * n)
    return np.ascontiguousarray(words), np.ascontiguousarray(byte.astype(np.uint8).reshape(k // 512, 16, n))


def unpack_weight(words, scales, fmt):
    g, _, n = scales.shape
    words = np.ascontiguousarray(words).reshape(g, 128, n, -1)
    if fmt == "e4m3":
        vals = words.view(ml_dtypes.float8_e4m3fn).astype(np.float64)
    else:
        nib = np.empty((g, 128, n, 4), np.uint8)
        nib[..., 0::2] = words & 0xF
        nib[..., 1::2] = words >> 4
        vals = E2M1[nib]
    vals = vals * np.repeat(np.exp2(scales.astype(np.float64) - 127.0), 8, axis=1)[..., None]
    return vals.transpose(0, 1, 3, 2).reshape(g * 512, n)


def gelu(v):
    return 0.5 * v * (1.0 + np.tanh(np.sqrt(2.0 / np.pi) * (v + 0.044715 * v**3)))


K, K2, T, TB, S, P, H, N = 1024, 512, 4096, 2048, 1024, 512, 1024, 512

def setup_inputs():
    n = np.random.standard_normal
    s, s2, u = mx_kscale(K)[:, None], mx_kscale(K2)[:, None], mx_kscale(H)[:, None]
    d = {}
    d["tab_words"], d["tab_scales"] = pack_weight(n((K, T)) * s, "e4m3")
    d["tab2_words"], d["tab2_scales"] = pack_weight(n((K2, TB)) * s2, "e4m3")
    d["offs"] = striped(np.random.permutation(T)[:S])
    d["offs2"] = striped(np.random.permutation(TB)[:P])
    d["pos1"] = striped(np.random.permutation(S)[:P])
    d["w1"] = (2.5 * n((K, H)) / K ** 0.5 / s).astype(np.float32)
    d["gain"] = (np.exp(0.3 * n(H)) * u[:, 0]).astype(np.float32)
    d["w2_words"], d["w2_scales"] = pack_weight(n((K2, H)) / K2 ** 0.5 / s2 * u.T, "e4m3")
    d["usual"] = (0.7 * n(H) * u[:, 0]).astype(np.float32)
    d["wgs"] = np.exp(0.3 * n((128, P))).astype(np.float32)
    d["w3_words"], d["w3_scales"] = pack_weight(n((H, N)) / H ** 0.5 / u, "e2m1")
    d["w4"] = (n((H, N)) / H ** 0.5 / u).astype(np.float32)
    return d

def reference(tab_words, tab_scales, tab2_words, tab2_scales, offs, offs2, pos1, w1, gain,
              w2_words, w2_scales, usual, wgs, w3_words, w3_scales, w4):
    v = unpack_weight(tab_words, tab_scales, "e4m3")[:, unstriped(offs)]
    v2 = unpack_weight(tab2_words, tab2_scales, "e4m3")[:, unstriped(offs2)]
    w2 = unpack_weight(w2_words, w2_scales, "e4m3")
    w3 = unpack_weight(w3_words, w3_scales, "e2m1")
    f = mxq(f64(w1), 0, "e4m3").T @ v
    a = f64(gain)[:, None] * np.log(1.0 + np.abs(f))
    b = (w2.T @ v2) - f64(usual)[:, None]
    placed = np.zeros((H, S))
    placed[:, unstriped(pos1)] = np.tile(f64(wgs), (H // 128, 1)) * b
    z = a + placed
    whole = w3.T @ mxq(z, 0, "e4m3")
    alone = mxq(f64(w4), 0, "e4m3").T @ mxq(placed, 0, "e4m3")
    return np.abs(whole - alone)

@@ -1,0 +1,287 @@
+from contextlib import ExitStack
+
+import concourse.mybir as mybir
+
+K, K2, T, TB, S, NP, H, N = 1024, 512, 4096, 2048, 1024, 512, 1024, 512
+FLOPS = 2 * (K * H * S + K2 * H * NP + 2 * H * N * S)
+
+F32 = mybir.dt.float32
+BF16 = mybir.dt.bfloat16
+I32 = mybir.dt.int32
+U32 = mybir.dt.uint32
+U16 = mybir.dt.uint16
+U8 = mybir.dt.uint8
+FP8X4 = mybir.dt.float8_e4m3fn_x4
+FP4X4 = mybir.dt.float4_e2m1fn_x4
+ACT = mybir.ActivationFunctionType
+ALU = mybir.AluOpType
+
+P = 128
+W = 512
+EARLY = 3
+
+
+def tile_list_supervision_intensity_scores_kernel(
+    tc, tab_words, tab_scales, tab2_words, tab2_scales, offs, offs2, pos1, w1, gain,
+    w2_words, w2_scales, usual, wgs, w3_words, w3_scales, w4, out,
+):
+    nc = tc.nc
+    with ExitStack() as ctx:
+        keep = ctx.enter_context(tc.tile_pool(name="keep", bufs=1))
+        ring = ctx.enter_context(tc.tile_pool(name="ring", bufs=1))
+        psum = ctx.enter_context(tc.psum_pool(name="psum", bufs=4))
+
+        offs_t = keep.tile([P, S // 16], U16, name="offs_t")
+        offs2_t = keep.tile([P, NP // 16], U16, name="offs2_t")
+        pos_t = keep.tile([P, NP // 16], U16, name="pos_t")
+
+        def slot(tag, shape, dtype, name):
+            return ring.tile(shape, dtype, name=name, tag=tag, bufs=1, align_bytes=64)
+
+        tab2w = slot("c", [P, TB], U32, "tab2w")
+        tab2s = slot("d", [P, TB], U8, "tab2s")
+        w2raw = slot("a", [P, H], I32, "w2raw")
+        w2sraw = slot("b", [P, H], U8, "w2sraw")
+        usual_t = keep.tile([P, 2, 8], F32, name="usual_t")
+        pages = [keep.tile([P, S], F32, name=f"page{k}", align_bytes=64) for k in range(4)]
+
+        def words(ap):
+            return ap.rearrange("p n t -> p (n t)").bitcast(I32)
+
+        nc.gpsimd.memset(w2sraw[:].bitcast(I32), 0)
+        nc.gpsimd.memset(tab2s[:].bitcast(I32), 0)
+        for k in range(4):
+            nc.vector.memset(pages[k][:], 0.0)
+
+        nc.sync.dma_start(offs2_t[:], offs2)
+        nc.sync.dma_start(pos_t[:], pos1)
+        nc.sync.dma_start(offs_t[:], offs)
+        nc.sync.dma_start(usual_t[:, :, 0:4], usual.rearrange("(b p t) -> p b t", b=2, t=4))
+        nc.sync.dma_start(w2raw[:], words(w2_words[0]))
+        nc.sync.dma_start(tab2w[:].bitcast(I32), words(tab2_words[0]))
+        for q in range(4):
+            nc.sync.dma_start(w2sraw[32 * q : 32 * q + 4, :].bitcast(I32), w2_scales[0, 4 * q : 4 * q + 4, :].bitcast(I32))
+        for q in range(4):
+            queue = nc.gpsimd if q < 2 else nc.sync
+            queue.dma_start(tab2s[32 * q : 32 * q + 4, :].bitcast(I32), tab2_scales[0, 4 * q : 4 * q + 4, :].bitcast(I32))
+
+        def load_raw(raw, src, a, b):
+            nc.sync.dma_start(raw, src[W * a : W * (a + 1), W * b : W * (b + 1)].rearrange("(p i) c -> p i c", i=4))
+            return raw
+
+        w2p = [slot(tag, [P, W], I32, "w2p") for tag in ("p4", "f")]
+        w2sp = [slot(tag, [P, W], U8, "w2sp") for tag in ("e", "g")]
+        for b in range(2):
+            nc.vector.tensor_copy(
+                w2p[b][:].rearrange("p (t g m) -> p g t m", t=4, m=4),
+                w2raw[:, W * b : W * (b + 1)].rearrange("p (g m t) -> p g t m", t=4, m=4))
+        wg = slot("a", [P, 4, NP], F32, "wg")
+        for q in (0, 2, 1, 3):
+            nc.sync.dma_start(wg[32 * q : 32 * q + 32, :, :], wgs.rearrange("(p t) j -> p t j", t=4))
+        for b in range(2):
+            nc.vector.tensor_copy(
+                w2sp[b][:].rearrange("p (t m) -> p t m", t=4),
+                w2sraw[:, W * b : W * (b + 1)].rearrange("p (m t) -> p t m", t=4))
+
+        gv2 = keep.tile([P, NP], U32, name="gv2", align_bytes=64)
+        gs2 = slot("h", [P, NP], U8, "gs2")
+        nc.vector.tensor_copy(gv2[:], tab2w[:].indirect(offs2_t[:]))
+        nc.vector.tensor_copy(gs2[:], tab2s[:].indirect(offs2_t[:]))
+
+        w1raw = {}
+        for a, tag in enumerate(("b", "c")):
+            w1raw[a, 0] = load_raw(slot(tag, [P, 4, W], F32, "raw")[:], w1, a, 0)
+        pair = slot("d", [P, 2, 4, W], F32, "pair")
+        for a in range(2):
+            w1raw[a, 1] = load_raw(pair[:, a, :, :], w1, a, 1)
+
+        def interviews(k):
+            b, t = divmod(k, 4)
+            cols = slice(P * t, P * (t + 1))
+            acc = psum.tile([P, W], F32, name="fin", tag="fin")
+            nc.tensor.matmul_mx(acc[:], lhsT=w2p[b][:, cols].bitcast(FP8X4), lhsT_scale=w2sp[b][:, cols],
+                                rhs=gv2[:].bitcast(FP8X4), rhs_scale=gs2[:], start=True, stop=True)
+            return acc
+
+        def place(k, acc, nb):
+            b, t = divmod(k, 4)
+            nc.scalar.activation(nb, acc[:], ACT.Identity, bias=usual_t[:, b, t : t + 1], scale=-1.0)
+            nc.vector.tensor_tensor(pages[k][:].indirect(pos_t[:]), nb, wg[:, t, :], ALU.mult)
+
+        def clear_page(k):
+            page = slot(f"p{k}", [P, S], F32, f"page{k}")
+            nc.gpsimd.memset(page[:], 0.0)
+            pages.append(page)
+
+        def stage_tile(width):
+            st = ring.tile([P, 4 * W], BF16, name="stage", tag="stage", bufs=6, align_bytes=64)
+            return st[:, 0 : 4 * width]
+
+        def operand(tag, bufs):
+            codes = ring.tile([P, W], U32, name=tag + "c", tag=tag + "c", bufs=bufs, align_bytes=64)
+            scales = ring.tile([P, W], U8, name=tag + "s", tag=tag + "s", bufs=bufs, align_bytes=64)
+            return codes, scales
+
+        def quantise(stage, dest, cols=slice(0, W)):
+            nc.vector.quantize_mx(out=dest[0][:, cols].bitcast(FP8X4), scales=dest[1][:, cols], in_=stage)
+            return dest
+
+        def cast_w1(a, b):
+            st = stage_tile(W)
+            nc.scalar.copy(st.rearrange("p (t m i) -> p m i t", t=4, i=4),
+                           w1raw[a, b].rearrange("p i (m t) -> p m i t", t=4))
+            return st
+
+        def weave(copy, src):
+            st = stage_tile(src.shape[2])
+            copy(st.rearrange("p (g c t) -> p g t c", t=4, c=4), src.rearrange("p t (g c) -> p g t c", c=4))
+            return st
+
+        gv = {}
+        gs = {}
+
+        def gather(h):
+            lst = offs_t[:, 32 * h : 32 * (h + 1)]
+            gv[0, h] = keep.tile([P, W], U32, name=f"gv0{h}", align_bytes=64)
+            nc.vector.tensor_copy(gv[0, h][:], tabw[0][:].indirect(lst))
+            gs[h] = keep.tile([P, W], U8, name=f"gs{h}", align_bytes=64)
+            nc.vector.tensor_copy(gs[h][:], tabs[:].indirect(lst))
+            gv[1, h] = keep.tile([P, W], U32, name=f"gv1{h}", align_bytes=64)
+            nc.vector.tensor_copy(gv[1, h][:], tabw[1][:].indirect(lst))
+
+        accs_b = [interviews(k) for k in range(4)]
+        tabs = slot("e", [P, T], U8, "tabs")
+        nc.gpsimd.memset(tabs[:].bitcast(I32), 0)
+        for q in range(4):
+            nc.sync.dma_start(tabs[32 * q : 32 * q + 8, :].bitcast(I32), tab_scales[:, 4 * q : 4 * q + 4, :].bitcast(I32))
+        clear_page(4)
+        for k in range(EARLY):
+            place(k, accs_b[k], slot(f"p{5 + k}", [P, W], F32, "nb")[:])
+            clear_page(5 + k)
+        w1q = {}
+        tabw = []
+        for a, tag in enumerate(("b", "c")):
+            w1q[a, 0] = quantise(cast_w1(a, 0), operand("w1", 4))
+            tw = slot(tag, [P, T], U32, "tabw")
+            nc.sync.dma_start(tw[:].bitcast(I32), words(tab_words[a]))
+            tabw.append(tw)
+        for a in range(2):
+            w1q[a, 1] = quantise(cast_w1(a, 1), operand("w1", 4))
+        pair = slot("d", [P, 2, 4, W], F32, "pair")
+        w4raw = [load_raw(pair[:, b, :, :], w4, b, 0) for b in range(2)]
+        gather(0)
+        gather(1)
+
+        late = slot("c", [P, 8 - EARLY, W], F32, "late")
+        for k in range(EARLY, 8):
+            place(k, accs_b[k] if k < 4 else interviews(k), late[:, k - EARLY, :])
+
+        gain_t = slot("h", [P, 2, 8], F32, "gain_t")
+        nc.sync.dma_start(gain_t[:, :, 0:4], gain.rearrange("(b p t) -> p b t", b=2, t=4))
+        w3w = slot("f", [P, 2, 2 * N], U8, "w3w")
+        w3s = slot("g", [P, 2, N], U8, "w3s")
+        nc.gpsimd.memset(w3s[:].rearrange("p a n -> p (a n)").bitcast(I32), 0)
+        nc.sync.dma_start(w3w[:].bitcast(I32), w3_words.rearrange("a p c -> p a c").bitcast(I32))
+        for q in range(4):
+            nc.sync.dma_start(w3s[32 * q : 32 * q + 4, :, :].bitcast(I32),
+                              w3_scales[:, 4 * q : 4 * q + 4, :].rearrange("a r c -> r a c").bitcast(I32))
+
+        joined = []
+        for b in range(2):
+            jn = slot("bc"[b], [P, 4, S], F32, "joined")
+            for t in range(4):
+                nc.sync.dma_start(jn[:, t, :], pages[4 * b + t][:])
+            joined.append(jn)
+
+        logs = {}
+
+        def features(b, h):
+            for t in range(4):
+                acc = psum.tile([P, W], F32, name="acc", tag="acc")
+                cols = slice(P * t, P * (t + 1))
+                for a in range(2):
+                    codes, scales = w1q[a, b]
+                    nc.tensor.matmul_mx(acc[:], lhsT=codes[:, cols].bitcast(FP8X4), lhsT_scale=scales[:, cols],
+                                        rhs=gv[a, h][:].bitcast(FP8X4), rhs_scale=gs[h][4 * a : P, :],
+                                        start=(a == 0), stop=(a == 1))
+                mag = ring.tile([P, W], F32, name="mag", tag="mag", bufs=2, align_bytes=64)
+                nc.scalar.activation(mag[:], acc[:], ACT.Abs)
+                lg = ring.tile([P, W], F32, name="lg", tag="lg", bufs=14, align_bytes=64)
+                nc.scalar.activation(lg[:], mag[:], ACT.Ln, bias=1.0)
+                logs[b, h, t] = lg
+
+        zq = {(b, h): operand("z", 4) for h in range(2) for b in range(2)}
+        pq = {(b, h): operand("p", 4) for h in range(2) for b in range(2)}
+        w4q = {}
+
+        def whole_case(b, h, cols):
+            width = cols.stop - cols.start
+            zc = ring.tile([P, 4, W], BF16, name="sums", tag="sums", bufs=2, align_bytes=64)
+            for t in range(4):
+                nc.vector.scalar_tensor_tensor(zc[:, t, 0:width], logs[b, h, t][:, cols], gain_t[:, b, t : t + 1],
+                                               pages[4 * b + t][:, W * h + cols.start : W * h + cols.stop],
+                                               ALU.mult, ALU.subtract)
+            quantise(weave(nc.vector.tensor_copy, zc[:, :, 0:width]), zq[b, h], cols)
+
+        def interview_alone(b, h, cols):
+            quantise(weave(nc.scalar.copy, joined[b][:, :, W * h + cols.start : W * h + cols.stop]), pq[b, h], cols)
+
+        def banks(tag):
+            return [psum.tile([P, W], F32, name=tag, tag=tag) for nt in range(4)]
+
+        def products(h, cols, accs, b):
+            width = cols.stop - cols.start
+            for step, kind in ((2 * b, "p"), (2 * b + 1, "z")):
+                for nt in range(4):
+                    rows = slice(P * nt, P * (nt + 1))
+                    if kind == "p":
+                        lhs = w4q[b][0][:, rows].bitcast(FP8X4)
+                        lhs_s = w4q[b][1][:, rows]
+                        codes, scales = pq[b, h]
+                        n = width
+                    else:
+                        lhs = w3w[:, b, 2 * P * nt : 2 * P * (nt + 1)].bitcast(FP4X4)
+                        lhs_s = w3s[:, b, rows]
+                        codes, scales = zq[b, h]
+                        n = W if width == W else P
+                    for c in range(0, width, n):
+                        part = slice(cols.start + c, cols.start + c + n)
+                        nc.tensor.matmul_mx(accs[nt][:, c : c + n], lhsT=lhs, lhsT_scale=lhs_s,
+                                            rhs=codes[:, part].bitcast(FP8X4), rhs_scale=scales[:, part],
+                                            start=(step == 0), stop=(step == 3 and c + n == width))
+
+        def store(h, cols, accs):
+            width = cols.stop - cols.start
+            for nt in range(4):
+                res = ring.tile([P, W], F32, name="res", tag="res", bufs=4, align_bytes=64)
+                nc.scalar.activation(res[:, 0:width], accs[nt][:, 0:width], ACT.Abs)
+                nc.sync.dma_start(out[P * nt : P * (nt + 1), W * h + cols.start : W * h + cols.stop], res[:, 0:width])
+
+        full = slice(0, W)
+        halves = (slice(0, W // 2), slice(W // 2, W))
+        features(0, 0)
+        whole_case(0, 0, full)
+        features(1, 0)
+        whole_case(1, 0, full)
+        for b in range(2):
+            w4q[b] = quantise(weave(nc.scalar.copy, w4raw[b]), operand("w4", 2))
+        interview_alone(0, 0, full)
+        interview_alone(0, 1, full)
+        interview_alone(1, 0, full)
+        first = banks("fin")
+        for b in range(2):
+            products(0, full, first, b)
+        features(0, 1)
+        whole_case(0, 1, full)
+        features(1, 1)
+        second = banks("acc")
+        products(1, halves[0], second, 0)
+        store(0, full, first)
+        third = banks("fin")
+        products(1, halves[1], third, 0)
+        for cols, accs in zip(halves, (second, third)):
+            interview_alone(1, 1, cols)
+            whole_case(1, 1, cols)
+            products(1, cols, accs, 1)
+        store(1, halves[0], second)
+        store(1, halves[1], third)

@@ -48,10 +48,14 @@ def tile_list_supervision_intensity_scores_kernel(
         def words(ap):
             return ap.rearrange("p n t -> p (n t)").bitcast(I32)
 
-        nc.gpsimd.memset(w2sraw[:].bitcast(I32), 0)
-        nc.gpsimd.memset(tab2s[:].bitcast(I32), 0)
+        nc.vector.memset(w2sraw[:].bitcast(I32), 0)
+        nc.vector.memset(tab2s[:].bitcast(I32), 0)
+        tabs = keep.tile([P, T], U8, name="tabs", align_bytes=64)
+        nc.vector.memset(tabs[:].bitcast(I32), 0)
         for k in range(4):
             nc.vector.memset(pages[k][:], 0.0)
+        warm = keep.tile([P, 8], F32, name="warm")
+        nc.scalar.activation(warm[:, 0:1], pages[0][:, 0:1], ACT.Ln, bias=1.0)
 
         nc.sync.dma_start(offs2_t[:], offs2)
         nc.sync.dma_start(pos_t[:], pos1)
@@ -64,12 +68,14 @@ def tile_list_supervision_intensity_scores_kernel(
         for q in range(4):
             queue = nc.gpsimd if q < 2 else nc.sync
             queue.dma_start(tab2s[32 * q : 32 * q + 4, :].bitcast(I32), tab2_scales[0, 4 * q : 4 * q + 4, :].bitcast(I32))
+        for q in range(4):
+            nc.gpsimd.dma_start(tabs[32 * q : 32 * q + 8, :].bitcast(I32), tab_scales[:, 4 * q : 4 * q + 4, :].bitcast(I32))
 
-        def load_raw(raw, src, a, b):
-            nc.sync.dma_start(raw, src[W * a : W * (a + 1), W * b : W * (b + 1)].rearrange("(p i) c -> p i c", i=4))
+        def load_raw(raw, src, a):
+            nc.sync.dma_start(raw, src[W * a : W * (a + 1), :].rearrange("(p i) c -> p i c", i=4))
             return raw
 
-        w2p = [slot(tag, [P, W], I32, "w2p") for tag in ("p4", "f")]
+        w2p = [slot(tag, [P, W], I32, "w2p") for tag in ("i", "f")]
         w2sp = [slot(tag, [P, W], U8, "w2sp") for tag in ("e", "g")]
         for b in range(2):
             nc.vector.tensor_copy(
@@ -77,7 +83,8 @@ def tile_list_supervision_intensity_scores_kernel(
                 w2raw[:, W * b : W * (b + 1)].rearrange("p (g m t) -> p g t m", t=4, m=4))
         wg = slot("a", [P, 4, NP], F32, "wg")
         for q in (0, 2, 1, 3):
-            nc.sync.dma_start(wg[32 * q : 32 * q + 32, :, :], wgs.rearrange("(p t) j -> p t j", t=4))
+            queue = nc.sync if q < 2 else nc.scalar
+            queue.dma_start(wg[32 * q : 32 * q + 32, :, :], wgs.rearrange("(p t) j -> p t j", t=4))
         for b in range(2):
             nc.vector.tensor_copy(
                 w2sp[b][:].rearrange("p (t m) -> p t m", t=4),
@@ -88,12 +95,7 @@ def tile_list_supervision_intensity_scores_kernel(
         nc.vector.tensor_copy(gv2[:], tab2w[:].indirect(offs2_t[:]))
         nc.vector.tensor_copy(gs2[:], tab2s[:].indirect(offs2_t[:]))
 
-        w1raw = {}
-        for a, tag in enumerate(("b", "c")):
-            w1raw[a, 0] = load_raw(slot(tag, [P, 4, W], F32, "raw")[:], w1, a, 0)
-        pair = slot("d", [P, 2, 4, W], F32, "pair")
-        for a in range(2):
-            w1raw[a, 1] = load_raw(pair[:, a, :, :], w1, a, 1)
+        w1raw = [load_raw(slot(tag, [P, 4, H], F32, "raw")[:], w1, a) for a, tag in enumerate("bc")]
 
         def interviews(k):
             b, t = divmod(k, 4)
@@ -108,8 +110,8 @@ def tile_list_supervision_intensity_scores_kernel(
             nc.scalar.activation(nb, acc[:], ACT.Identity, bias=usual_t[:, b, t : t + 1], scale=-1.0)
             nc.vector.tensor_tensor(pages[k][:].indirect(pos_t[:]), nb, wg[:, t, :], ALU.mult)
 
-        def clear_page(k):
-            page = slot(f"p{k}", [P, S], F32, f"page{k}")
+        def clear_page(k, tag):
+            page = slot(tag, [P, S], F32, f"page{k}")
             nc.gpsimd.memset(page[:], 0.0)
             pages.append(page)
 
@@ -129,50 +131,44 @@ def tile_list_supervision_intensity_scores_kernel(
         def cast_w1(a, b):
             st = stage_tile(W)
             nc.scalar.copy(st.rearrange("p (t m i) -> p m i t", t=4, i=4),
-                           w1raw[a, b].rearrange("p i (m t) -> p m i t", t=4))
+                           w1raw[a][:, :, W * b : W * (b + 1)].rearrange("p i (m t) -> p m i t", t=4))
             return st
 
-        def weave(copy, src):
-            st = stage_tile(src.shape[2])
+        def weave(copy, src, st):
             copy(st.rearrange("p (g c t) -> p g t c", t=4, c=4), src.rearrange("p t (g c) -> p g t c", c=4))
             return st
 
         gv = {}
-        gs = {}
 
         def gather(h):
             lst = offs_t[:, 32 * h : 32 * (h + 1)]
             gv[0, h] = keep.tile([P, W], U32, name=f"gv0{h}", align_bytes=64)
             nc.vector.tensor_copy(gv[0, h][:], tabw[0][:].indirect(lst))
-            gs[h] = keep.tile([P, W], U8, name=f"gs{h}", align_bytes=64)
-            nc.vector.tensor_copy(gs[h][:], tabs[:].indirect(lst))
+            nc.vector.tensor_copy(gs[:, W * h : W * (h + 1)], tabs[:].indirect(lst))
             gv[1, h] = keep.tile([P, W], U32, name=f"gv1{h}", align_bytes=64)
             nc.vector.tensor_copy(gv[1, h][:], tabw[1][:].indirect(lst))
 
         accs_b = [interviews(k) for k in range(4)]
-        tabs = slot("e", [P, T], U8, "tabs")
-        nc.gpsimd.memset(tabs[:].bitcast(I32), 0)
-        for q in range(4):
-            nc.sync.dma_start(tabs[32 * q : 32 * q + 8, :].bitcast(I32), tab_scales[:, 4 * q : 4 * q + 4, :].bitcast(I32))
-        clear_page(4)
-        for k in range(EARLY):
-            place(k, accs_b[k], slot(f"p{5 + k}", [P, W], F32, "nb")[:])
-            clear_page(5 + k)
-        w1q = {}
         tabw = []
-        for a, tag in enumerate(("b", "c")):
-            w1q[a, 0] = quantise(cast_w1(a, 0), operand("w1", 4))
+        for a, tag in enumerate("de"):
             tw = slot(tag, [P, T], U32, "tabw")
             nc.sync.dma_start(tw[:].bitcast(I32), words(tab_words[a]))
             tabw.append(tw)
+        gs = slot("i", [P, S], U8, "gs")
+        for k in range(EARLY):
+            place(k, accs_b[k], slot(f"p{4 + k}", [P, W], F32, "nb")[:])
+            clear_page(4 + k, f"p{4 + k}")
+        w1q = {}
         for a in range(2):
-            w1q[a, 1] = quantise(cast_w1(a, 1), operand("w1", 4))
-        pair = slot("d", [P, 2, 4, W], F32, "pair")
-        w4raw = [load_raw(pair[:, b, :, :], w4, b, 0) for b in range(2)]
+            for b in range(2):
+                w1q[a, b] = quantise(cast_w1(a, b), operand("w1", 4))
+        clear_page(7, "c")
+        pair = slot("b", [P, 2, 4, W], F32, "pair")
+        w4raw = [load_raw(pair[:, b, :, :], w4, b) for b in range(2)]
         gather(0)
         gather(1)
 
-        late = slot("c", [P, 8 - EARLY, W], F32, "late")
+        late = slot("e", [P, 8 - EARLY, W], F32, "late")
         for k in range(EARLY, 8):
             place(k, accs_b[k] if k < 4 else interviews(k), late[:, k - EARLY, :])
 
@@ -188,7 +184,7 @@ def tile_list_supervision_intensity_scores_kernel(
 
         joined = []
         for b in range(2):
-            jn = slot("bc"[b], [P, 4, S], F32, "joined")
+            jn = slot("de"[b], [P, 4, S], F32, "joined")
             for t in range(4):
                 nc.sync.dma_start(jn[:, t, :], pages[4 * b + t][:])
             joined.append(jn)
@@ -197,16 +193,16 @@ def tile_list_supervision_intensity_scores_kernel(
 
         def features(b, h):
             for t in range(4):
-                acc = psum.tile([P, W], F32, name="acc", tag="acc")
+                acc = psum.tile([P, W], F32, name="acc", tag=("acc", "fin")[b])
                 cols = slice(P * t, P * (t + 1))
                 for a in range(2):
                     codes, scales = w1q[a, b]
                     nc.tensor.matmul_mx(acc[:], lhsT=codes[:, cols].bitcast(FP8X4), lhsT_scale=scales[:, cols],
-                                        rhs=gv[a, h][:].bitcast(FP8X4), rhs_scale=gs[h][4 * a : P, :],
+                                        rhs=gv[a, h][:].bitcast(FP8X4), rhs_scale=gs[4 * a : P, W * h : W * (h + 1)],
                                         start=(a == 0), stop=(a == 1))
-                mag = ring.tile([P, W], F32, name="mag", tag="mag", bufs=2, align_bytes=64)
+                mag = ring.tile([P, W], F32, name="mag", tag="mag", bufs=3, align_bytes=64)
                 nc.scalar.activation(mag[:], acc[:], ACT.Abs)
-                lg = ring.tile([P, W], F32, name="lg", tag="lg", bufs=14, align_bytes=64)
+                lg = ring.tile([P, W], F32, name="lg", tag="lg", bufs=12, align_bytes=64)
                 nc.scalar.activation(lg[:], mag[:], ACT.Ln, bias=1.0)
                 logs[b, h, t] = lg
 
@@ -217,14 +213,26 @@ def tile_list_supervision_intensity_scores_kernel(
         def whole_case(b, h, cols):
             width = cols.stop - cols.start
             zc = ring.tile([P, 4, W], BF16, name="sums", tag="sums", bufs=2, align_bytes=64)
-            for t in range(4):
-                nc.vector.scalar_tensor_tensor(zc[:, t, 0:width], logs[b, h, t][:, cols], gain_t[:, b, t : t + 1],
-                                               pages[4 * b + t][:, W * h + cols.start : W * h + cols.stop],
+
+            def add(t, part):
+                nc.vector.scalar_tensor_tensor(zc[:, t, part], logs[b, h, t][:, part], gain_t[:, b, t : t + 1],
+                                               pages[4 * b + t][:, W * h + part.start : W * h + part.stop],
                                                ALU.mult, ALU.subtract)
-            quantise(weave(nc.vector.tensor_copy, zc[:, :, 0:width]), zq[b, h], cols)
+
+            middle = cols.start + width // 2
+            parts = (slice(cols.start, middle), slice(middle, cols.stop))
+            for t in range(3):
+                add(t, cols)
+            for part in parts:
+                add(3, part)
+            st = stage_tile(W)
+            woven = [weave(nc.vector.tensor_copy, zc[:, :, part], st[:, 4 * part.start : 4 * part.stop]) for part in parts]
+            for part, piece in zip(parts, woven):
+                quantise(piece, zq[b, h], part)
 
         def interview_alone(b, h, cols):
-            quantise(weave(nc.scalar.copy, joined[b][:, :, W * h + cols.start : W * h + cols.stop]), pq[b, h], cols)
+            quantise(weave(nc.scalar.copy, joined[b][:, :, W * h + cols.start : W * h + cols.stop],
+                           stage_tile(cols.stop - cols.start)), pq[b, h], cols)
 
         def banks(tag):
             return [psum.tile([P, W], F32, name=tag, tag=tag) for nt in range(4)]
@@ -264,20 +272,20 @@ def tile_list_supervision_intensity_scores_kernel(
         features(1, 0)
         whole_case(1, 0, full)
         for b in range(2):
-            w4q[b] = quantise(weave(nc.scalar.copy, w4raw[b]), operand("w4", 2))
+            w4q[b] = quantise(weave(nc.scalar.copy, w4raw[b], stage_tile(W)), operand("w4", 2))
         interview_alone(0, 0, full)
         interview_alone(0, 1, full)
         interview_alone(1, 0, full)
-        first = banks("fin")
-        for b in range(2):
-            products(0, full, first, b)
         features(0, 1)
         whole_case(0, 1, full)
         features(1, 1)
-        second = banks("acc")
+        first = banks("acc")
+        for b in range(2):
+            products(0, full, first, b)
+        second = banks("fin")
         products(1, halves[0], second, 0)
         store(0, full, first)
-        third = banks("fin")
+        third = banks("acc")
         products(1, halves[1], third, 0)
         for cols, accs in zip(halves, (second, third)):
             interview_alone(1, 1, cols)

@@ -48,6 +48,8 @@ def tile_list_supervision_intensity_scores_kernel(
         def words(ap):
             return ap.rearrange("p n t -> p (n t)").bitcast(I32)
 
+        last_page = keep.tile([P, S], F32, name="page7", align_bytes=64)
+        nc.gpsimd.memset(last_page[:], 0.0)
         nc.vector.memset(w2sraw[:].bitcast(I32), 0)
         nc.vector.memset(tab2s[:].bitcast(I32), 0)
         tabs = keep.tile([P, T], U8, name="tabs", align_bytes=64)
@@ -112,7 +114,7 @@ def tile_list_supervision_intensity_scores_kernel(
 
         def clear_page(k, tag):
             page = slot(tag, [P, S], F32, f"page{k}")
-            nc.gpsimd.memset(page[:], 0.0)
+            nc.vector.memset(page[:], 0.0)
             pages.append(page)
 
         def stage_tile(width):
@@ -162,7 +164,7 @@ def tile_list_supervision_intensity_scores_kernel(
         for a in range(2):
             for b in range(2):
                 w1q[a, b] = quantise(cast_w1(a, b), operand("w1", 4))
-        clear_page(7, "c")
+        pages.append(last_page)
         pair = slot("b", [P, 2, 4, W], F32, "pair")
         w4raw = [load_raw(pair[:, b, :, :], w4, b) for b in range(2)]
         gather(0)
@@ -184,9 +186,11 @@ def tile_list_supervision_intensity_scores_kernel(
 
         joined = []
         for b in range(2):
-            jn = slot("de"[b], [P, 4, S], F32, "joined")
-            for t in range(4):
+            jn = slot("dc"[b], [P, 4, S], F32, "joined")
+            for t in range(3):
                 nc.sync.dma_start(jn[:, t, :], pages[4 * b + t][:])
+            for h in range(2):
+                nc.sync.dma_start(jn[:, 3, W * h : W * (h + 1)], pages[4 * b + 3][:, W * h : W * (h + 1)])
             joined.append(jn)
 
         logs = {}

@@ -38,20 +38,17 @@ def tile_list_supervision_intensity_scores_kernel(
         def slot(tag, shape, dtype, name):
             return ring.tile(shape, dtype, name=name, tag=tag, bufs=1, align_bytes=64)
 
-        tab2w = slot("c", [P, TB], U32, "tab2w")
-        tab2s = slot("d", [P, TB], U8, "tab2s")
+        tab2w = slot("b", [P, TB], U32, "tab2w")
+        tab2s = slot("c", [P, TB], U8, "tab2s")
         w2raw = slot("a", [P, H], I32, "w2raw")
-        w2sraw = slot("b", [P, H], U8, "w2sraw")
-        usual_t = keep.tile([P, 2, 8], F32, name="usual_t")
-        pages = [keep.tile([P, S], F32, name=f"page{k}", align_bytes=64) for k in range(4)]
+        w2sraw = slot("d", [P, H], U8, "w2sraw")
+        pages = {k: keep.tile([P, S], F32, name=f"page{k}", align_bytes=64) for k in range(4)}
 
         def words(ap):
             return ap.rearrange("p n t -> p (n t)").bitcast(I32)
 
-        last_page = keep.tile([P, S], F32, name="page7", align_bytes=64)
-        nc.gpsimd.memset(last_page[:], 0.0)
-        nc.vector.memset(w2sraw[:].bitcast(I32), 0)
         nc.vector.memset(tab2s[:].bitcast(I32), 0)
+        nc.vector.memset(w2sraw[:].bitcast(I32), 0)
         tabs = keep.tile([P, T], U8, name="tabs", align_bytes=64)
         nc.vector.memset(tabs[:].bitcast(I32), 0)
         for k in range(4):
@@ -62,14 +59,12 @@ def tile_list_supervision_intensity_scores_kernel(
         nc.sync.dma_start(offs2_t[:], offs2)
         nc.sync.dma_start(pos_t[:], pos1)
         nc.sync.dma_start(offs_t[:], offs)
-        nc.sync.dma_start(usual_t[:, :, 0:4], usual.rearrange("(b p t) -> p b t", b=2, t=4))
         nc.sync.dma_start(w2raw[:], words(w2_words[0]))
         nc.sync.dma_start(tab2w[:].bitcast(I32), words(tab2_words[0]))
         for q in range(4):
-            nc.sync.dma_start(w2sraw[32 * q : 32 * q + 4, :].bitcast(I32), w2_scales[0, 4 * q : 4 * q + 4, :].bitcast(I32))
+            nc.sync.dma_start(tab2s[32 * q : 32 * q + 4, :].bitcast(I32), tab2_scales[0, 4 * q : 4 * q + 4, :].bitcast(I32))
         for q in range(4):
-            queue = nc.gpsimd if q < 2 else nc.sync
-            queue.dma_start(tab2s[32 * q : 32 * q + 4, :].bitcast(I32), tab2_scales[0, 4 * q : 4 * q + 4, :].bitcast(I32))
+            nc.sync.dma_start(w2sraw[32 * q : 32 * q + 4, :].bitcast(I32), w2_scales[0, 4 * q : 4 * q + 4, :].bitcast(I32))
         for q in range(4):
             nc.gpsimd.dma_start(tabs[32 * q : 32 * q + 8, :].bitcast(I32), tab_scales[:, 4 * q : 4 * q + 4, :].bitcast(I32))
 
@@ -77,25 +72,29 @@ def tile_list_supervision_intensity_scores_kernel(
             nc.sync.dma_start(raw, src[W * a : W * (a + 1), :].rearrange("(p i) c -> p i c", i=4))
             return raw
 
-        w2p = [slot(tag, [P, W], I32, "w2p") for tag in ("i", "f")]
+        w2p = [slot(tag, [P, 2 * P], I32, "w2p") for tag in ("p4", "p7", "f0", "f1")]
         w2sp = [slot(tag, [P, W], U8, "w2sp") for tag in ("e", "g")]
-        for b in range(2):
+        for u in range(4):
+            b, t = u // 2, 2 * (u % 2)
             nc.vector.tensor_copy(
-                w2p[b][:].rearrange("p (t g m) -> p g t m", t=4, m=4),
-                w2raw[:, W * b : W * (b + 1)].rearrange("p (g m t) -> p g t m", t=4, m=4))
-        wg = slot("a", [P, 4, NP], F32, "wg")
+                w2p[u][:].rearrange("p (t g m) -> p g t m", t=2, m=4),
+                w2raw[:, W * b : W * (b + 1)].rearrange("p (g m t) -> p g t m", t=4, m=4)[:, :, t : t + 2, :])
+        factors = slot("a", [P, 4 * NP + 16], F32, "factors")
+        wg = factors[:, 0 : 4 * NP].rearrange("p (t j) -> p t j", t=4)
+        usual_t = factors[:, 4 * NP : 4 * NP + 16].rearrange("p (b t) -> p b t", b=2)
+        nc.sync.dma_start(usual_t[:, :, 0:4], usual.rearrange("(b p t) -> p b t", b=2, t=4))
         for q in (0, 2, 1, 3):
             queue = nc.sync if q < 2 else nc.scalar
             queue.dma_start(wg[32 * q : 32 * q + 32, :, :], wgs.rearrange("(p t) j -> p t j", t=4))
-        for b in range(2):
-            nc.vector.tensor_copy(
-                w2sp[b][:].rearrange("p (t m) -> p t m", t=4),
-                w2sraw[:, W * b : W * (b + 1)].rearrange("p (m t) -> p t m", t=4))
 
         gv2 = keep.tile([P, NP], U32, name="gv2", align_bytes=64)
         gs2 = slot("h", [P, NP], U8, "gs2")
         nc.vector.tensor_copy(gv2[:], tab2w[:].indirect(offs2_t[:]))
         nc.vector.tensor_copy(gs2[:], tab2s[:].indirect(offs2_t[:]))
+        for b in range(2):
+            nc.vector.tensor_copy(
+                w2sp[b][:].rearrange("p (t m) -> p t m", t=4),
+                w2sraw[:, W * b : W * (b + 1)].rearrange("p (m t) -> p t m", t=4))
 
         w1raw = [load_raw(slot(tag, [P, 4, H], F32, "raw")[:], w1, a) for a, tag in enumerate("bc")]
 
@@ -103,7 +102,7 @@ def tile_list_supervision_intensity_scores_kernel(
             b, t = divmod(k, 4)
             cols = slice(P * t, P * (t + 1))
             acc = psum.tile([P, W], F32, name="fin", tag="fin")
-            nc.tensor.matmul_mx(acc[:], lhsT=w2p[b][:, cols].bitcast(FP8X4), lhsT_scale=w2sp[b][:, cols],
+            nc.tensor.matmul_mx(acc[:], lhsT=w2p[k // 2][:, P * (k % 2) : P * (k % 2 + 1)].bitcast(FP8X4), lhsT_scale=w2sp[b][:, cols],
                                 rhs=gv2[:].bitcast(FP8X4), rhs_scale=gs2[:], start=True, stop=True)
             return acc
 
@@ -114,8 +113,8 @@ def tile_list_supervision_intensity_scores_kernel(
 
         def clear_page(k, tag):
             page = slot(tag, [P, S], F32, f"page{k}")
-            nc.vector.memset(page[:], 0.0)
-            pages.append(page)
+            nc.gpsimd.memset(page[:], 0.0)
+            pages[k] = page
 
         def stage_tile(width):
             st = ring.tile([P, 4 * W], BF16, name="stage", tag="stage", bufs=6, align_bytes=64)
@@ -156,15 +155,17 @@ def tile_list_supervision_intensity_scores_kernel(
             tw = slot(tag, [P, T], U32, "tabw")
             nc.sync.dma_start(tw[:].bitcast(I32), words(tab_words[a]))
             tabw.append(tw)
+        clear_page(4, "p4")
+        clear_page(7, "p7")
+        for k, tag in enumerate(("i", "p5", "p6")):
+            place(k, accs_b[k], slot(tag, [P, W], F32, "nb")[:])
         gs = slot("i", [P, S], U8, "gs")
-        for k in range(EARLY):
-            place(k, accs_b[k], slot(f"p{4 + k}", [P, W], F32, "nb")[:])
-            clear_page(4 + k, f"p{4 + k}")
+        clear_page(5, "p5")
+        clear_page(6, "p6")
         w1q = {}
         for a in range(2):
             for b in range(2):
                 w1q[a, b] = quantise(cast_w1(a, b), operand("w1", 4))
-        pages.append(last_page)
         pair = slot("b", [P, 2, 4, W], F32, "pair")
         w4raw = [load_raw(pair[:, b, :, :], w4, b) for b in range(2)]
         gather(0)
@@ -176,9 +177,9 @@ def tile_list_supervision_intensity_scores_kernel(
 
         gain_t = slot("h", [P, 2, 8], F32, "gain_t")
         nc.sync.dma_start(gain_t[:, :, 0:4], gain.rearrange("(b p t) -> p b t", b=2, t=4))
-        w3w = slot("f", [P, 2, 2 * N], U8, "w3w")
+        w3w = slot("f1", [P, 2, 2 * N], U8, "w3w")
         w3s = slot("g", [P, 2, N], U8, "w3s")
-        nc.gpsimd.memset(w3s[:].rearrange("p a n -> p (a n)").bitcast(I32), 0)
+        nc.vector.memset(w3s[:].rearrange("p a n -> p (a n)").bitcast(I32), 0)
         nc.sync.dma_start(w3w[:].bitcast(I32), w3_words.rearrange("a p c -> p a c").bitcast(I32))
         for q in range(4):
             nc.sync.dma_start(w3s[32 * q : 32 * q + 4, :, :].bitcast(I32),
@@ -234,9 +235,8 @@ def tile_list_supervision_intensity_scores_kernel(
             for part, piece in zip(parts, woven):
                 quantise(piece, zq[b, h], part)
 
-        def interview_alone(b, h, cols):
-            quantise(weave(nc.scalar.copy, joined[b][:, :, W * h + cols.start : W * h + cols.stop],
-                           stage_tile(cols.stop - cols.start)), pq[b, h], cols)
+        def interview_alone(b, h):
+            quantise(weave(nc.scalar.copy, joined[b][:, :, W * h : W * (h + 1)], stage_tile(W)), pq[b, h])
 
         def banks(tag):
             return [psum.tile([P, W], F32, name=tag, tag=tag) for nt in range(4)]
@@ -277,11 +277,12 @@ def tile_list_supervision_intensity_scores_kernel(
         whole_case(1, 0, full)
         for b in range(2):
             w4q[b] = quantise(weave(nc.scalar.copy, w4raw[b], stage_tile(W)), operand("w4", 2))
-        interview_alone(0, 0, full)
-        interview_alone(0, 1, full)
-        interview_alone(1, 0, full)
+        interview_alone(0, 0)
+        interview_alone(0, 1)
+        interview_alone(1, 0)
         features(0, 1)
         whole_case(0, 1, full)
+        interview_alone(1, 1)
         features(1, 1)
         first = banks("acc")
         for b in range(2):
@@ -292,7 +293,6 @@ def tile_list_supervision_intensity_scores_kernel(
         third = banks("acc")
         products(1, halves[1], third, 0)
         for cols, accs in zip(halves, (second, third)):
-            interview_alone(1, 1, cols)
             whole_case(1, 1, cols)
             products(1, cols, accs, 1)
         store(1, halves[0], second)

from contextlib import ExitStack

import concourse.mybir as mybir

K, K2, T, TB, S, NP, H, N = 1024, 512, 4096, 2048, 1024, 512, 1024, 512
FLOPS = 2 * (K * H * S + K2 * H * NP + 2 * H * N * S)

F32 = mybir.dt.float32
BF16 = mybir.dt.bfloat16
I32 = mybir.dt.int32
U32 = mybir.dt.uint32
U16 = mybir.dt.uint16
U8 = mybir.dt.uint8
FP8X4 = mybir.dt.float8_e4m3fn_x4
FP4X4 = mybir.dt.float4_e2m1fn_x4
ACT = mybir.ActivationFunctionType
ALU = mybir.AluOpType

P = 128
W = 512
EARLY = 3


def tile_list_supervision_intensity_scores_kernel(
    tc, tab_words, tab_scales, tab2_words, tab2_scales, offs, offs2, pos1, w1, gain,
    w2_words, w2_scales, usual, wgs, w3_words, w3_scales, w4, out,
):
    nc = tc.nc
    with ExitStack() as ctx:
        keep = ctx.enter_context(tc.tile_pool(name="keep", bufs=1))
        ring = ctx.enter_context(tc.tile_pool(name="ring", bufs=1))
        psum = ctx.enter_context(tc.psum_pool(name="psum", bufs=4))

        offs_t = keep.tile([P, S // 16], U16, name="offs_t")
        offs2_t = keep.tile([P, NP // 16], U16, name="offs2_t")
        pos_t = keep.tile([P, NP // 16], U16, name="pos_t")

        def slot(tag, shape, dtype, name):
            return ring.tile(shape, dtype, name=name, tag=tag, bufs=1, align_bytes=64)

        tab2w = slot("b", [P, TB], U32, "tab2w")
        tab2s = slot("c", [P, TB], U8, "tab2s")
        w2raw = slot("a", [P, H], I32, "w2raw")
        w2sraw = slot("d", [P, H], U8, "w2sraw")
        pages = {k: keep.tile([P, S], F32, name=f"page{k}", align_bytes=64) for k in range(4)}

        def words(ap):
            return ap.rearrange("p n t -> p (n t)").bitcast(I32)

        nc.vector.memset(tab2s[:].bitcast(I32), 0)
        nc.vector.memset(w2sraw[:].bitcast(I32), 0)
        tabs = keep.tile([P, T], U8, name="tabs", align_bytes=64)
        nc.vector.memset(tabs[:].bitcast(I32), 0)
        for k in range(4):
            nc.vector.memset(pages[k][:], 0.0)
        warm = keep.tile([P, 8], F32, name="warm")
        nc.scalar.activation(warm[:, 0:1], pages[0][:, 0:1], ACT.Ln, bias=1.0)

        nc.sync.dma_start(offs2_t[:], offs2)
        nc.sync.dma_start(pos_t[:], pos1)
        nc.sync.dma_start(offs_t[:], offs)
        nc.sync.dma_start(w2raw[:], words(w2_words[0]))
        nc.sync.dma_start(tab2w[:].bitcast(I32), words(tab2_words[0]))
        for q in range(4):
            nc.sync.dma_start(tab2s[32 * q : 32 * q + 4, :].bitcast(I32), tab2_scales[0, 4 * q : 4 * q + 4, :].bitcast(I32))
        for q in range(4):
            nc.sync.dma_start(w2sraw[32 * q : 32 * q + 4, :].bitcast(I32), w2_scales[0, 4 * q : 4 * q + 4, :].bitcast(I32))
        for q in range(4):
            nc.gpsimd.dma_start(tabs[32 * q : 32 * q + 8, :].bitcast(I32), tab_scales[:, 4 * q : 4 * q + 4, :].bitcast(I32))

        def load_raw(raw, src, a):
            nc.sync.dma_start(raw, src[W * a : W * (a + 1), :].rearrange("(p i) c -> p i c", i=4))
            return raw

        w2p = [slot(tag, [P, 2 * P], I32, "w2p") for tag in ("p4", "p7", "f0", "f1")]
        w2sp = [slot(tag, [P, W], U8, "w2sp") for tag in ("e", "g")]
        for u in range(4):
            b, t = u // 2, 2 * (u % 2)
            nc.vector.tensor_copy(
                w2p[u][:].rearrange("p (t g m) -> p g t m", t=2, m=4),
                w2raw[:, W * b : W * (b + 1)].rearrange("p (g m t) -> p g t m", t=4, m=4)[:, :, t : t + 2, :])
        factors = slot("a", [P, 4 * NP + 16], F32, "factors")
        wg = factors[:, 0 : 4 * NP].rearrange("p (t j) -> p t j", t=4)
        usual_t = factors[:, 4 * NP : 4 * NP + 16].rearrange("p (b t) -> p b t", b=2)
        nc.sync.dma_start(usual_t[:, :, 0:4], usual.rearrange("(b p t) -> p b t", b=2, t=4))
        for q in (0, 2, 1, 3):
            queue = nc.sync if q < 2 else nc.scalar
            queue.dma_start(wg[32 * q : 32 * q + 32, :, :], wgs.rearrange("(p t) j -> p t j", t=4))

        gv2 = keep.tile([P, NP], U32, name="gv2", align_bytes=64)
        gs2 = slot("h", [P, NP], U8, "gs2")
        nc.vector.tensor_copy(gv2[:], tab2w[:].indirect(offs2_t[:]))
        nc.vector.tensor_copy(gs2[:], tab2s[:].indirect(offs2_t[:]))
        for b in range(2):
            nc.vector.tensor_copy(
                w2sp[b][:].rearrange("p (t m) -> p t m", t=4),
                w2sraw[:, W * b : W * (b + 1)].rearrange("p (m t) -> p t m", t=4))

        w1raw = [load_raw(slot(tag, [P, 4, H], F32, "raw")[:], w1, a) for a, tag in enumerate("bc")]

        def interviews(k):
            b, t = divmod(k, 4)
            cols = slice(P * t, P * (t + 1))
            acc = psum.tile([P, W], F32, name="fin", tag="fin")
            nc.tensor.matmul_mx(acc[:], lhsT=w2p[k // 2][:, P * (k % 2) : P * (k % 2 + 1)].bitcast(FP8X4), lhsT_scale=w2sp[b][:, cols],
                                rhs=gv2[:].bitcast(FP8X4), rhs_scale=gs2[:], start=True, stop=True)
            return acc

        def place(k, acc, nb):
            b, t = divmod(k, 4)
            nc.scalar.activation(nb, acc[:], ACT.Identity, bias=usual_t[:, b, t : t + 1], scale=-1.0)
            nc.vector.tensor_tensor(pages[k][:].indirect(pos_t[:]), nb, wg[:, t, :], ALU.mult)

        def clear_page(k, tag):
            page = slot(tag, [P, S], F32, f"page{k}")
            nc.gpsimd.memset(page[:], 0.0)
            pages[k] = page

        def stage_tile(width):
            st = ring.tile([P, 4 * W], BF16, name="stage", tag="stage", bufs=6, align_bytes=64)
            return st[:, 0 : 4 * width]

        def operand(tag, bufs):
            codes = ring.tile([P, W], U32, name=tag + "c", tag=tag + "c", bufs=bufs, align_bytes=64)
            scales = ring.tile([P, W], U8, name=tag + "s", tag=tag + "s", bufs=bufs, align_bytes=64)
            return codes, scales

        def quantise(stage, dest, cols=slice(0, W)):
            nc.vector.quantize_mx(out=dest[0][:, cols].bitcast(FP8X4), scales=dest[1][:, cols], in_=stage)
            return dest

        def cast_w1(a, b):
            st = stage_tile(W)
            nc.scalar.copy(st.rearrange("p (t m i) -> p m i t", t=4, i=4),
                           w1raw[a][:, :, W * b : W * (b + 1)].rearrange("p i (m t) -> p m i t", t=4))
            return st

        def weave(copy, src, st):
            copy(st.rearrange("p (g c t) -> p g t c", t=4, c=4), src.rearrange("p t (g c) -> p g t c", c=4))
            return st

        gv = {}

        def gather(h):
            lst = offs_t[:, 32 * h : 32 * (h + 1)]
            gv[0, h] = keep.tile([P, W], U32, name=f"gv0{h}", align_bytes=64)
            nc.vector.tensor_copy(gv[0, h][:], tabw[0][:].indirect(lst))
            nc.vector.tensor_copy(gs[:, W * h : W * (h + 1)], tabs[:].indirect(lst))
            gv[1, h] = keep.tile([P, W], U32, name=f"gv1{h}", align_bytes=64)
            nc.vector.tensor_copy(gv[1, h][:], tabw[1][:].indirect(lst))

        accs_b = [interviews(k) for k in range(4)]
        tabw = []
        for a, tag in enumerate("de"):
            tw = slot(tag, [P, T], U32, "tabw")
            nc.sync.dma_start(tw[:].bitcast(I32), words(tab_words[a]))
            tabw.append(tw)
        clear_page(4, "p4")
        clear_page(7, "p7")
        for k, tag in enumerate(("i", "p5", "p6")):
            place(k, accs_b[k], slot(tag, [P, W], F32, "nb")[:])
        gs = slot("i", [P, S], U8, "gs")
        clear_page(5, "p5")
        clear_page(6, "p6")
        w1q = {}
        for a in range(2):
            for b in range(2):
                w1q[a, b] = quantise(cast_w1(a, b), operand("w1", 4))
        pair = slot("b", [P, 2, 4, W], F32, "pair")
        w4raw = [load_raw(pair[:, b, :, :], w4, b) for b in range(2)]
        gather(0)
        gather(1)

        late = slot("e", [P, 8 - EARLY, W], F32, "late")
        for k in range(EARLY, 8):
            place(k, accs_b[k] if k < 4 else interviews(k), late[:, k - EARLY, :])

        gain_t = slot("h", [P, 2, 8], F32, "gain_t")
        nc.sync.dma_start(gain_t[:, :, 0:4], gain.rearrange("(b p t) -> p b t", b=2, t=4))
        w3w = slot("f1", [P, 2, 2 * N], U8, "w3w")
        w3s = slot("g", [P, 2, N], U8, "w3s")
        nc.vector.memset(w3s[:].rearrange("p a n -> p (a n)").bitcast(I32), 0)
        nc.sync.dma_start(w3w[:].bitcast(I32), w3_words.rearrange("a p c -> p a c").bitcast(I32))
        for q in range(4):
            nc.sync.dma_start(w3s[32 * q : 32 * q + 4, :, :].bitcast(I32),
                              w3_scales[:, 4 * q : 4 * q + 4, :].rearrange("a r c -> r a c").bitcast(I32))

        joined = []
        for b in range(2):
            jn = slot("dc"[b], [P, 4, S], F32, "joined")
            for t in range(3):
                nc.sync.dma_start(jn[:, t, :], pages[4 * b + t][:])
            for h in range(2):
                nc.sync.dma_start(jn[:, 3, W * h : W * (h + 1)], pages[4 * b + 3][:, W * h : W * (h + 1)])
            joined.append(jn)

        logs = {}

        def features(b, h):
            for t in range(4):
                acc = psum.tile([P, W], F32, name="acc", tag=("acc", "fin")[b])
                cols = slice(P * t, P * (t + 1))
                for a in range(2):
                    codes, scales = w1q[a, b]
                    nc.tensor.matmul_mx(acc[:], lhsT=codes[:, cols].bitcast(FP8X4), lhsT_scale=scales[:, cols],
                                        rhs=gv[a, h][:].bitcast(FP8X4), rhs_scale=gs[4 * a : P, W * h : W * (h + 1)],
                                        start=(a == 0), stop=(a == 1))
                mag = ring.tile([P, W], F32, name="mag", tag="mag", bufs=3, align_bytes=64)
                nc.scalar.activation(mag[:], acc[:], ACT.Abs)
                lg = ring.tile([P, W], F32, name="lg", tag="lg", bufs=12, align_bytes=64)
                nc.scalar.activation(lg[:], mag[:], ACT.Ln, bias=1.0)
                logs[b, h, t] = lg

        zq = {(b, h): operand("z", 4) for h in range(2) for b in range(2)}
        pq = {(b, h): operand("p", 4) for h in range(2) for b in range(2)}
        w4q = {}

        def whole_case(b, h, cols):
            width = cols.stop - cols.start
            zc = ring.tile([P, 4, W], BF16, name="sums", tag="sums", bufs=2, align_bytes=64)

            def add(t, part):
                nc.vector.scalar_tensor_tensor(zc[:, t, part], logs[b, h, t][:, part], gain_t[:, b, t : t + 1],
                                               pages[4 * b + t][:, W * h + part.start : W * h + part.stop],
                                               ALU.mult, ALU.subtract)

            middle = cols.start + width // 2
            parts = (slice(cols.start, middle), slice(middle, cols.stop))
            for t in range(3):
                add(t, cols)
            for part in parts:
                add(3, part)
            st = stage_tile(W)
            woven = [weave(nc.vector.tensor_copy, zc[:, :, part], st[:, 4 * part.start : 4 * part.stop]) for part in parts]
            for part, piece in zip(parts, woven):
                quantise(piece, zq[b, h], part)

        def interview_alone(b, h):
            quantise(weave(nc.scalar.copy, joined[b][:, :, W * h : W * (h + 1)], stage_tile(W)), pq[b, h])

        def banks(tag):
            return [psum.tile([P, W], F32, name=tag, tag=tag) for nt in range(4)]

        def products(h, cols, accs, b):
            width = cols.stop - cols.start
            for step, kind in ((2 * b, "p"), (2 * b + 1, "z")):
                for nt in range(4):
                    rows = slice(P * nt, P * (nt + 1))
                    if kind == "p":
                        lhs = w4q[b][0][:, rows].bitcast(FP8X4)
                        lhs_s = w4q[b][1][:, rows]
                        codes, scales = pq[b, h]
                        n = width
                    else:
                        lhs = w3w[:, b, 2 * P * nt : 2 * P * (nt + 1)].bitcast(FP4X4)
                        lhs_s = w3s[:, b, rows]
                        codes, scales = zq[b, h]
                        n = W if width == W else P
                    for c in range(0, width, n):
                        part = slice(cols.start + c, cols.start + c + n)
                        nc.tensor.matmul_mx(accs[nt][:, c : c + n], lhsT=lhs, lhsT_scale=lhs_s,
                                            rhs=codes[:, part].bitcast(FP8X4), rhs_scale=scales[:, part],
                                            start=(step == 0), stop=(step == 3 and c + n == width))

        def store(h, cols, accs):
            width = cols.stop - cols.start
            for nt in range(4):
                res = ring.tile([P, W], F32, name="res", tag="res", bufs=4, align_bytes=64)
                nc.scalar.activation(res[:, 0:width], accs[nt][:, 0:width], ACT.Abs)
                nc.sync.dma_start(out[P * nt : P * (nt + 1), W * h + cols.start : W * h + cols.stop], res[:, 0:width])

        full = slice(0, W)
        halves = (slice(0, W // 2), slice(W // 2, W))
        features(0, 0)
        whole_case(0, 0, full)
        features(1, 0)
        whole_case(1, 0, full)
        for b in range(2):
            w4q[b] = quantise(weave(nc.scalar.copy, w4raw[b], stage_tile(W)), operand("w4", 2))
        interview_alone(0, 0)
        interview_alone(0, 1)
        interview_alone(1, 0)
        features(0, 1)
        whole_case(0, 1, full)
        interview_alone(1, 1)
        features(1, 1)
        first = banks("acc")
        for b in range(2):
            products(0, full, first, b)
        second = banks("fin")
        products(1, halves[0], second, 0)
        store(0, full, first)
        third = banks("acc")
        products(1, halves[1], third, 0)
        for cols, accs in zip(halves, (second, third)):
            whole_case(1, 1, cols)
            products(1, cols, accs, 1)
        store(1, halves[0], second)
        store(1, halves[1], third)
